import numpy as np
import ml_dtypes


def mxq(x, axis, fmt="e4m3"):
    dtype, down = {"e4m3": (ml_dtypes.float8_e4m3fn, 7), "e5m2": (ml_dtypes.float8_e5m2, 14)}[fmt]
    v = np.moveaxis(np.asarray(x, np.float32).astype(ml_dtypes.bfloat16).astype(np.float64), axis, -1)
    blocks = v.reshape(v.shape[:-1] + (-1, 32))
    amax = np.abs(blocks).max(-1, keepdims=True)
    byte = np.maximum(np.where(amax > 0, np.frexp(amax)[1] - 1 + 127, 0) - down, 1)
    scale = np.exp2(byte - 127.0)
    codes = (blocks / scale).astype(np.float32).astype(dtype).astype(np.float64)
    return np.moveaxis((codes * scale).reshape(v.shape), -1, axis)


WIDE = False


def mx_kscale(k):
    if not WIDE:
        return np.ones(k)
    levels = np.array([30, -30])
    if k % 512:
        return np.exp2(np.random.permutation(np.resize(levels, k // 32))).repeat(32)
    a = np.empty((k // 512, 16))
    for p in range(k // 512):
        a[p, :8] = np.random.permutation(np.resize(levels, 8))
        for g in range(8):
            far = levels[np.abs(levels - a[p, g]) >= 10]
            a[p, g + 8] = far[np.random.randint(len(far))]
    return np.exp2(a.ravel()).repeat(32)


BF16 = ml_dtypes.bfloat16


def bf(x):
    return np.asarray(x, np.float32).astype(BF16)


def f64(x):
    return np.asarray(x).astype(np.float64)


E2M1 = np.array([0.0, 0.5, 1.0, 1.5, 2.0, 3.0, 4.0, 6.0, -0.0, -0.5, -1.0, -1.5, -2.0, -3.0, -4.0, -6.0])


def pack_weight(w, fmt):
    k, n = w.shape
    w = f64(bf(w)).reshape(k // 32, 32, n)
    amax = np.abs(w).max(1)
    if fmt in ("e4m3", "e5m2"):
        byte = np.frexp(amax)[1] - 1 + 127 - (7 if fmt == "e4m3" else 14)
    else:
        mant, ex = np.frexp(amax / 6.0)
        byte = np.where(mant > 0.5, ex, ex - 1) + 127
    byte = np.clip(np.where(amax > 0, byte, 1), 1, 254)
    scaled = (w * np.exp2(127.0 - byte)[:, None, :]).reshape(k, n).astype(np.float32)
    by_word = np.ascontiguousarray(scaled.reshape(k // 512, 128, 4, n).transpose(0, 1, 3, 2))
    if fmt in ("e4m3", "e5m2"):
        words = by_word.astype(ml_dtypes.float8_e4m3fn if fmt == "e4m3" else ml_dtypes.float8_e5m2).view(np.uint8)
    else:
        c = by_word.astype(ml_dtypes.float4_e2m1fn).view(np.uint8) & 0xF
        words = c[..., 0::2] | (c[..., 1::2] << 4)
    return np.ascontiguousarray(words), np.ascontiguousarray(byte.astype(np.uint8).reshape(k // 512, 16, n))


def unpack_weight(words, scales, fmt):
    g, p, n, _ = words.shape
    if fmt in ("e4m3", "e5m2"):
        vals = np.ascontiguousarray(words).view(ml_dtypes.float8_e4m3fn if fmt == "e4m3" else ml_dtypes.float8_e5m2).astype(np.float64)
    else:
        nib = np.empty((g, p, n, 4), np.uint8)
        nib[..., 0::2] = words & 0xF
        nib[..., 1::2] = words >> 4
        vals = E2M1[nib]
    vals = vals * np.repeat(np.exp2(scales.astype(np.float64) - 127.0), 8, axis=1)[..., None]
    return vals.transpose(0, 1, 3, 2).reshape(g * 512, n)

def planes(Y):
    n, m = Y.shape
    b = f64(bf(Y)).reshape(n // 32, 32, m)
    amax = np.abs(b).max(1)
    byte = np.clip(np.where(amax > 0, np.frexp(amax)[1] - 1 + 127 - 7, 1), 1, 254)
    codes = (b * np.exp2(127.0 - byte)[:, None, :]).reshape(n, m).astype(np.float32).astype(ml_dtypes.float8_e4m3fn).view(np.uint8)
    words = codes.reshape(n // 512, 128, 4, m).transpose(0, 1, 3, 2)
    return np.ascontiguousarray(words), np.ascontiguousarray(byte.astype(np.uint8).reshape(n // 512, 16, m))


P, K, F, ROWS, COLS, D = 1024, 2048, 1024, 32, 64, 2

def setup_inputs():
    s = mx_kscale(K)
    rows = np.repeat(np.arange(ROWS), COLS)
    cols = np.tile(np.arange(COLS), ROWS)
    d2 = (rows - ROWS * np.random.rand(P, 1)) ** 2 + (cols - COLS * np.random.rand(P, 1)) ** 2
    width = 4.0 + 4.0 * np.random.rand(P, 1)
    w = (1.0 + d2 / width ** 2) ** -1.5
    w = w / w.sum(axis=1, keepdims=True)
    gx = np.random.randn(K)
    gy = 0.5 * gx + np.random.randn(K)
    motion = np.random.randn(D, D, F)
    ramp = (cols / COLS - 0.5)[:, None]
    u = motion[0, 0] + motion[0, 1] * ramp
    v = motion[1, 0] + motion[1, 1] * ramp
    it = 2.0 * np.random.standard_t(3.0, (K, F)) - gx[:, None] * u - gy[:, None] * v
    G = np.concatenate([gx[:, None] * it, gy[:, None] * it], axis=1)
    g_words, g_scales = pack_weight(G / s[:, None], "e5m2")
    sxx = (w * gx * gx).sum(axis=1)
    sxy = (w * gx * gy).sum(axis=1)
    syy = (w * gy * gy).sum(axis=1)
    gain = np.exp(0.8 * np.random.randn(P)) / (sxx * syy - sxy * sxy)
    return {"window": bf(w * s), "g_words": g_words, "g_scales": g_scales,
            "sxy": bf(sxy), "sopp": bf(np.stack([syy, sxx], axis=1)), "gain": bf(gain)}

def reference(window, g_words, g_scales, sxy, sopp, gain):
    b = (mxq(f64(window), 1, "e4m3") @ unpack_weight(g_words, g_scales, "e5m2")).reshape(P, D, F)
    y = (f64(sxy)[:, None, None] * b[:, ::-1] - f64(sopp)[:, :, None] * b) * f64(gain)[:, None, None]
    Y = y.reshape(P, D * F)
    words, scales = planes(Y)
    return y, words, scales

@@ -1,0 +1,269 @@
+from contextlib import ExitStack
+
+import concourse.mybir as mybir
+from concourse.masks import make_identity
+
+WINDOWS, PIXELS, FRAMES = 1024, 2048, 1024
+FLOPS = 2 * WINDOWS * PIXELS * 2 * FRAMES
+
+F32 = mybir.dt.float32
+BF16 = mybir.dt.bfloat16
+I32 = mybir.dt.int32
+U32 = mybir.dt.uint32
+U8 = mybir.dt.uint8
+E4M3X4 = mybir.dt.float8_e4m3fn_x4
+E5M2X4 = mybir.dt.float8_e5m2_x4
+ALU = mybir.AluOpType
+ACT = mybir.ActivationFunctionType
+
+P = 128
+PACK = 4
+GROUPS = 2
+PASSES = 4
+CHUNK = 256
+CHUNKS = FRAMES // CHUNK
+N = 2 * CHUNK
+UNITS = GROUPS * CHUNKS
+STEPS = UNITS * PACK
+EARLY = (FRAMES + CHUNK) // 4
+ROW = 2 * FRAMES // 4
+
+TURN_BEFORE = {0: [0], 1: [1, 2], 2: [3], 8: [4], 10: [5], 12: [6], 14: [7]}
+SORT_BEFORE = {3: 1, 4: 2, 8: 3}
+VECTOR_COLS = (0, 192)
+SCALAR_COLS = [(192, 304), (304, 416), (416, 512)]
+
+
+def tile_lucas_kanade_window_flow_k2_kernel(tc, window, g_words, g_scales, sxy, sopp, gain, out_0, out_1, out_2):
+    nc = tc.nc
+    with ExitStack() as ctx:
+        keep = ctx.enter_context(tc.tile_pool(name="keep", bufs=1))
+        ring = ctx.enter_context(tc.tile_pool(name="ring", bufs=3))
+        turn_ps = ctx.enter_context(tc.psum_pool(name="turn_ps", bufs=4))
+        sum_ps = ctx.enter_context(tc.psum_pool(name="sum_ps", bufs=4))
+        ctx.enter_context(tc.manual_schedule())
+
+        w_raw = [keep.tile([P, PIXELS], BF16, name="w_raw%d" % j) for j in range(GROUPS * PACK)]
+        w_codes = [keep.tile([P, PASSES * P], U32, name="w_codes%d" % j, align_bytes=64) for j in range(GROUPS * PACK)]
+        w_scales = [keep.tile([P, PASSES * P], U8, name="w_scales%d" % j, align_bytes=64) for j in range(GROUPS * PACK)]
+        g_codes = [keep.tile([P, PASSES, N], U32, name="g_codes%d" % q, align_bytes=64) for q in range(CHUNKS)]
+        g_planes = [keep.tile([P, PASSES, N], U8, name="g_planes%d" % q, align_bytes=64) for q in range(CHUNKS)]
+        g_rows = keep.tile([P, PASSES, ROW], I32, name="g_rows")
+        y = [keep.tile([P, PACK, N], F32, name="y%d" % u) for u in range(UNITS)]
+        y_codes = [keep.tile([P, N], U32, name="y_codes%d" % u, align_bytes=64) for u in range(UNITS)]
+        y_planes = [keep.tile([P, 2 * FRAMES], U8, name="y_planes%d" % g, align_bytes=64) for g in range(GROUPS)]
+        ident = keep.tile([P, P], F32, name="ident")
+        sxy_sb = keep.tile([P, GROUPS, PACK], BF16, name="sxy_sb")
+        gain_sb = keep.tile([P, GROUPS, PACK], BF16, name="gain_sb")
+        sopp_sb = keep.tile([P, GROUPS, PACK * 2], BF16, name="sopp_sb")
+        minus_gain = keep.tile([P, GROUPS * PACK], F32, name="minus_gain")
+        cross = keep.tile([P, GROUPS * PACK], F32, name="cross")
+        own = keep.tile([P, 2, GROUPS * PACK], F32, name="own")
+
+        words_in = g_words.rearrange("k p n t -> k p (n t)").bitcast(I32)
+        rows_in = g_scales.bitcast(I32).rearrange("k (Q r) n -> r Q k n", r=4)
+        y_out = out_0.rearrange("(g p t) c f -> g p (t c) f", g=GROUPS, t=PACK)
+        words_out = out_1.rearrange("g p m t -> g p (m t)").bitcast(I32).rearrange("g p (c f) -> g p c f", c=2)
+        rows_out = out_2.bitcast(I32).rearrange("g (Q r) (c f) -> g r Q c f", r=4, c=2)
+
+        def load_window(j):
+            g, t = divmod(j, PACK)
+            rows = window.rearrange("(g m t) k -> g t m k", g=GROUPS, t=PACK)
+            nc.sync.dma_start(out=w_raw[j][:], in_=rows[g, t])
+
+        def load_pass(q, k):
+            src = words_in[k].rearrange("p (c f) -> p c f", c=2)[:, :, q * CHUNK : (q + 1) * CHUNK]
+            nc.sync.dma_start(out=g_codes[q][:, k, :].bitcast(I32).rearrange("p (c f) -> p c f", c=2), in_=src)
+
+        def load_chunk(q):
+            for c in range(2):
+                first = c * FRAMES + q * CHUNK
+                src = words_in.rearrange("k p n -> p k n")[:, :, first : first + CHUNK]
+                nc.sync.dma_start(out=g_codes[q][:].bitcast(I32)[:, :, c * CHUNK : (c + 1) * CHUNK], in_=src)
+
+        def load_scale_rows(first, last):
+            for r in range(4):
+                nc.sync.dma_start(out=g_rows[r:P:32, :, first:last], in_=rows_in[r][:, :, first:last])
+
+        nc.scalar.dma_start(out=gain_sb[:], in_=gain.rearrange("(g p t) -> p g t", g=GROUPS, t=PACK))
+        nc.vector.memset(g_rows[:, :, 0:EARLY], 0)
+        nc.vector.memset(g_rows[:, :, EARLY:ROW], 0)
+        make_identity(nc, ident[:])
+        nc.gpsimd.dma_start(out=sxy_sb[:], in_=sxy.rearrange("(g p t) -> p g t", g=GROUPS, t=PACK))
+        nc.gpsimd.dma_start(out=sopp_sb[:], in_=sopp.rearrange("(g p t) c -> p g (t c)", g=GROUPS, t=PACK))
+
+        load_window(0)
+        load_pass(0, 0)
+        load_scale_rows(0, EARLY)
+        for k in range(1, PASSES):
+            load_pass(0, k)
+        for j in range(1, PACK):
+            load_window(j)
+        load_chunk(1)
+        load_scale_rows(EARLY, ROW)
+        load_chunk(2)
+        load_window(4)
+        load_window(5)
+        load_chunk(3)
+        load_window(6)
+        load_window(7)
+
+        flat_gain = gain_sb[:].rearrange("p g t -> p (g t)")
+        nc.scalar.activation(out=minus_gain[:], in_=flat_gain, func=ACT.Copy, scale=-1.0)
+        nc.gpsimd.tensor_tensor(out=cross[:], in0=sxy_sb[:].rearrange("p g t -> p (g t)"), in1=flat_gain, op=ALU.mult)
+        sopp_by_c = sopp_sb[:].rearrange("p g (t c) -> p c (g t)", c=2)
+        for c in range(2):
+            nc.gpsimd.tensor_tensor(out=own[:, c, :], in0=sopp_by_c[:, c, :], in1=minus_gain[:], op=ALU.mult)
+
+        turned = {}
+        sums = {}
+        scaled = {}
+        rounded = {}
+
+        def turn(j):
+            words = w_raw[j][:].bitcast(F32)
+            for h in range(2):
+                bank = turn_ps.tile([P, 2, 2, P], F32, name="bank")
+                turned[j, h] = bank
+                for kk in range(2):
+                    k = 2 * h + kk
+                    for u in range(2):
+                        nc.tensor.transpose(bank[:, kk, u, :], words[:, 256 * k + u : 256 * (k + 1) : 2], ident[:])
+
+        def quantize_window(j, h):
+            grouped = ring.tile([P, 2 * P * PACK], BF16, name="grouped", align_bytes=64)
+            nc.scalar.copy(
+                out=grouped[:].bitcast(F32).rearrange("p (k m u) -> p k m u", k=2, u=2),
+                in_=turned[j, h][:].rearrange("p k u m -> p k m u"),
+            )
+            cols = slice(h * 2 * P, (h + 1) * 2 * P)
+            nc.vector.quantize_mx(out=w_codes[j][:, cols].bitcast(E4M3X4), scales=w_scales[j][:, cols], in_=grouped[:])
+
+        def sort_scales(q):
+            w = CHUNK // 4
+            nc.vector.tensor_copy(
+                out=g_planes[q][:].bitcast(I32).rearrange("p k (c f) -> p k c f", c=2),
+                in_=g_rows[:].rearrange("p k (c f) -> p k c f", c=2)[:, :, :, q * w : (q + 1) * w],
+            )
+
+        def multiply(s):
+            u, t = divmod(s, PACK)
+            g, q = divmod(u, CHUNKS)
+            j = g * PACK + t
+            acc = sum_ps.tile([P, N], F32, name="acc")
+            sums[s] = acc
+            for k in range(PASSES):
+                cols = slice(k * P, (k + 1) * P)
+                nc.tensor.matmul_mx(
+                    out=acc[:],
+                    lhsT=w_codes[j][:, cols].bitcast(E4M3X4),
+                    lhsT_scale=w_scales[j][:, cols],
+                    rhs=g_codes[q][:, k, :].bitcast(E5M2X4),
+                    rhs_scale=g_planes[q][:, k, :],
+                    start=(k == 0),
+                    stop=(k == PASSES - 1),
+                )
+
+        def scale_sums(s):
+            j = (s // (CHUNKS * PACK)) * PACK + s % PACK
+            crossed = ring.tile([P, N], F32, name="crossed")
+            scaled[s] = crossed
+            nc.scalar.activation(out=crossed[:], in_=sums[s][:], func=ACT.Copy, scale=cross[:, j : j + 1])
+
+        def solve(s):
+            u, t = divmod(s, PACK)
+            j = (u // CHUNKS) * PACK + t
+            for c in range(2):
+                nc.vector.scalar_tensor_tensor(
+                    out=y[u][:, t, c * CHUNK : (c + 1) * CHUNK],
+                    in0=sums[s][:, c * CHUNK : (c + 1) * CHUNK],
+                    scalar=own[:, c, j : j + 1],
+                    in1=scaled[s][:, (1 - c) * CHUNK : (2 - c) * CHUNK],
+                    op0=ALU.mult,
+                    op1=ALU.add,
+                )
+
+        def interleave(u, cols, copy):
+            if u not in rounded:
+                rounded[u] = ring.tile([P, N, PACK], BF16, name="rounded", align_bytes=64)
+            a, b = cols
+            copy(
+                out=rounded[u][:, a:b, :].rearrange("p (n i) t -> p n t i", i=4),
+                in_=y[u][:, :, a:b].rearrange("p t (n i) -> p n t i", i=4),
+            )
+
+        def quantize_y(u, c):
+            g, q = divmod(u, CHUNKS)
+            first = c * FRAMES + q * CHUNK
+            nc.vector.quantize_mx(
+                out=y_codes[u][:, c * CHUNK : (c + 1) * CHUNK].bitcast(E4M3X4),
+                scales=y_planes[g][:, first : first + CHUNK],
+                in_=rounded[u][:, c * CHUNK : (c + 1) * CHUNK, :].rearrange("p n t -> p (n t)"),
+            )
+
+        def store_y(u, t0, t1):
+            g, q = divmod(u, CHUNKS)
+            nc.sync.dma_start(
+                out=y_out[g][:, 2 * t0 : 2 * t1, q * CHUNK : (q + 1) * CHUNK],
+                in_=y[u][:, t0:t1, :].rearrange("p t (c f) -> p (t c) f", c=2),
+            )
+
+        def store_codes(u):
+            g, q = divmod(u, CHUNKS)
+            nc.sync.dma_start(
+                out=words_out[g][:, :, q * CHUNK : (q + 1) * CHUNK],
+                in_=y_codes[u][:].bitcast(I32).rearrange("p (c f) -> p c f", c=2),
+            )
+
+        def store_scale_rows(g, q0, q1, queues):
+            w = CHUNK // 4
+            plane = y_planes[g][:].bitcast(I32).rearrange("p (c f) -> p c f", c=2)
+            for r in range(4):
+                queues[r % len(queues)].dma_start(
+                    out=rows_out[g, r][:, :, q0 * w : q1 * w], in_=plane[r:P:32, :, q0 * w : q1 * w]
+                )
+
+        last = UNITS - 1
+        for s in range(STEPS + 1):
+            tiles = TURN_BEFORE.get(s, [])
+            for j in tiles:
+                turn(j)
+            u, phase = divmod(s - PACK - 1, PACK)
+            if s > 0:
+                scale_sums(s - 1)
+            if u >= 0 and phase < 3:
+                interleave(u, SCALAR_COLS[phase], nc.scalar.copy)
+            if s > 0:
+                solve(s - 1)
+            if u >= 0 and phase == 0:
+                interleave(u, VECTOR_COLS, nc.vector.tensor_copy)
+            if u >= 0 and phase in (1, 2):
+                quantize_y(u, phase - 1)
+            if s in SORT_BEFORE:
+                sort_scales(SORT_BEFORE[s])
+            for j in tiles:
+                for h in range(2):
+                    quantize_window(j, h)
+                    if (j, h) == (0, 0):
+                        sort_scales(0)
+            if s < STEPS:
+                multiply(s)
+            if s > 0 and s % PACK == 0 and s < STEPS:
+                store_y(s // PACK - 1, 0, PACK)
+            if s > last * PACK:
+                store_y(last, s - 1 - last * PACK, s - last * PACK)
+            if u >= 0 and phase == 2:
+                store_codes(u)
+                if u == CHUNKS - 1:
+                    store_scale_rows(0, 0, CHUNKS, [nc.sync])
+                if u == last - 1:
+                    store_scale_rows(1, 0, CHUNKS - 1, [nc.sync])
+
+        interleave(last, (0, 128), nc.scalar.copy)
+        interleave(last, (128, 256), nc.vector.tensor_copy)
+        interleave(last, (400, 512), nc.scalar.copy)
+        interleave(last, (256, 400), nc.vector.tensor_copy)
+        quantize_y(last, 0)
+        quantize_y(last, 1)
+        store_codes(last)
+        store_scale_rows(1, CHUNKS - 1, CHUNKS, [nc.sync, nc.scalar])

@@ -28,10 +28,16 @@ STEPS = UNITS * PACK
 EARLY = (FRAMES + CHUNK) // 4
 ROW = 2 * FRAMES // 4
 
-TURN_BEFORE = {0: [0], 1: [1, 2], 2: [3], 8: [4], 10: [5], 12: [6], 14: [7]}
-SORT_BEFORE = {3: 1, 4: 2, 8: 3}
-VECTOR_COLS = (0, 192)
-SCALAR_COLS = [(192, 304), (304, 416), (416, 512)]
+ORDER = [(0, 0)] + [(1, q) for q in range(CHUNKS)] + [(0, q) for q in range(1, CHUNKS)]
+FIRST = 3
+TURN_BEFORE = {2: [3], 3: [4], 4: [5], 5: [6], 6: [7]}
+SORT_WORDS = {1: [3], 2: [4], 3: [5], 4: [6], 5: [7]}
+GROUP_IN = TURN_BEFORE
+QUANTIZE_IN = TURN_BEFORE
+SORT_BEFORE = {4: 1, 8: 2, 12: 3}
+FINE_FROM = 16
+VECTOR_COLS = (0, 224)
+SCALAR_COLS = [(224, 320), (320, 416), (416, 512)]
 
 
 def tile_lucas_kanade_window_flow_k2_kernel(tc, window, g_words, g_scales, sxy, sopp, gain, out_0, out_1, out_2):
@@ -92,21 +98,17 @@ def tile_lucas_kanade_window_flow_k2_kernel(tc, window, g_words, g_scales, sxy, 
         nc.gpsimd.dma_start(out=sxy_sb[:], in_=sxy.rearrange("(g p t) -> p g t", g=GROUPS, t=PACK))
         nc.gpsimd.dma_start(out=sopp_sb[:], in_=sopp.rearrange("(g p t) c -> p g (t c)", g=GROUPS, t=PACK))
 
-        load_window(0)
-        load_pass(0, 0)
-        load_scale_rows(0, EARLY)
-        for k in range(1, PASSES):
-            load_pass(0, k)
-        for j in range(1, PACK):
+        for j in range(FIRST):
             load_window(j)
-        load_chunk(1)
+        load_scale_rows(0, EARLY)
+        for k in range(PASSES):
+            load_pass(0, k)
+        for j in range(FIRST, GROUPS * PACK):
+            load_window(j)
         load_scale_rows(EARLY, ROW)
+        load_chunk(1)
         load_chunk(2)
-        load_window(4)
-        load_window(5)
         load_chunk(3)
-        load_window(6)
-        load_window(7)
 
         flat_gain = gain_sb[:].rearrange("p g t -> p (g t)")
         nc.scalar.activation(out=minus_gain[:], in_=flat_gain, func=ACT.Copy, scale=-1.0)
@@ -115,29 +117,43 @@ def tile_lucas_kanade_window_flow_k2_kernel(tc, window, g_words, g_scales, sxy, 
         for c in range(2):
             nc.gpsimd.tensor_tensor(out=own[:, c, :], in0=sopp_by_c[:, c, :], in1=minus_gain[:], op=ALU.mult)
 
+        ordered = {}
         turned = {}
+        grouped = {}
         sums = {}
         scaled = {}
         rounded = {}
 
+        def sort_words(j):
+            words = w_raw[j][:].bitcast(F32).rearrange("m (h k n i u) -> m h k n u i", h=2, k=2, i=4, u=2)
+            for h in range(2):
+                by_parity = ring.tile([P, 2, 2, P], F32, name="by_parity", bufs=4)
+                ordered[j, h] = by_parity
+                nc.vector.tensor_copy(out=by_parity[:].rearrange("m k u (n i) -> m k n u i", i=4), in_=words[:, h])
+
         def turn(j):
-            words = w_raw[j][:].bitcast(F32)
             for h in range(2):
                 bank = turn_ps.tile([P, 2, 2, P], F32, name="bank")
                 turned[j, h] = bank
-                for kk in range(2):
-                    k = 2 * h + kk
+                for k in range(2):
                     for u in range(2):
-                        nc.tensor.transpose(bank[:, kk, u, :], words[:, 256 * k + u : 256 * (k + 1) : 2], ident[:])
+                        nc.tensor.transpose(bank[:, k, u, :], ordered[j, h][:, k, u, :], ident[:])
 
-        def quantize_window(j, h):
-            grouped = ring.tile([P, 2 * P * PACK], BF16, name="grouped", align_bytes=64)
-            nc.scalar.copy(
-                out=grouped[:].bitcast(F32).rearrange("p (k m u) -> p k m u", k=2, u=2),
-                in_=turned[j, h][:].rearrange("p k u m -> p k m u"),
-            )
-            cols = slice(h * 2 * P, (h + 1) * 2 * P)
-            nc.vector.quantize_mx(out=w_codes[j][:, cols].bitcast(E4M3X4), scales=w_scales[j][:, cols], in_=grouped[:])
+        def group_window(j):
+            for h in range(2):
+                fours = ring.tile([P, 2 * P * PACK], BF16, name="fours", align_bytes=64, bufs=4)
+                grouped[j, h] = fours
+                nc.scalar.copy(
+                    out=fours[:].bitcast(F32).rearrange("p (k m u) -> p k m u", k=2, u=2),
+                    in_=turned[j, h][:].rearrange("p k u m -> p k m u"),
+                )
+
+        def quantize_window(j):
+            for h in range(2):
+                cols = slice(h * 2 * P, (h + 1) * 2 * P)
+                nc.vector.quantize_mx(
+                    out=w_codes[j][:, cols].bitcast(E4M3X4), scales=w_scales[j][:, cols], in_=grouped[j, h][:]
+                )
 
         def sort_scales(q):
             w = CHUNK // 4
@@ -148,7 +164,7 @@ def tile_lucas_kanade_window_flow_k2_kernel(tc, window, g_words, g_scales, sxy, 
 
         def multiply(s):
             u, t = divmod(s, PACK)
-            g, q = divmod(u, CHUNKS)
+            g, q = ORDER[u]
             j = g * PACK + t
             acc = sum_ps.tile([P, N], F32, name="acc")
             sums[s] = acc
@@ -165,14 +181,14 @@ def tile_lucas_kanade_window_flow_k2_kernel(tc, window, g_words, g_scales, sxy, 
                 )
 
         def scale_sums(s):
-            j = (s // (CHUNKS * PACK)) * PACK + s % PACK
+            j = ORDER[s // PACK][0] * PACK + s % PACK
             crossed = ring.tile([P, N], F32, name="crossed")
             scaled[s] = crossed
             nc.scalar.activation(out=crossed[:], in_=sums[s][:], func=ACT.Copy, scale=cross[:, j : j + 1])
 
         def solve(s):
             u, t = divmod(s, PACK)
-            j = (u // CHUNKS) * PACK + t
+            j = ORDER[u][0] * PACK + t
             for c in range(2):
                 nc.vector.scalar_tensor_tensor(
                     out=y[u][:, t, c * CHUNK : (c + 1) * CHUNK],
@@ -192,27 +208,28 @@ def tile_lucas_kanade_window_flow_k2_kernel(tc, window, g_words, g_scales, sxy, 
                 in_=y[u][:, :, a:b].rearrange("p t (n i) -> p n t i", i=4),
             )
 
-        def quantize_y(u, c):
-            g, q = divmod(u, CHUNKS)
-            first = c * FRAMES + q * CHUNK
+        def quantize_y(u, a, b):
+            g, q = ORDER[u]
+            c, f = divmod(a, CHUNK)
+            first = c * FRAMES + q * CHUNK + f
             nc.vector.quantize_mx(
-                out=y_codes[u][:, c * CHUNK : (c + 1) * CHUNK].bitcast(E4M3X4),
-                scales=y_planes[g][:, first : first + CHUNK],
-                in_=rounded[u][:, c * CHUNK : (c + 1) * CHUNK, :].rearrange("p n t -> p (n t)"),
+                out=y_codes[u][:, a:b].bitcast(E4M3X4),
+                scales=y_planes[g][:, first : first + b - a],
+                in_=rounded[u][:, a:b, :].rearrange("p n t -> p (n t)"),
             )
 
         def store_y(u, t0, t1):
-            g, q = divmod(u, CHUNKS)
+            g, q = ORDER[u]
             nc.sync.dma_start(
                 out=y_out[g][:, 2 * t0 : 2 * t1, q * CHUNK : (q + 1) * CHUNK],
                 in_=y[u][:, t0:t1, :].rearrange("p t (c f) -> p (t c) f", c=2),
             )
 
-        def store_codes(u):
-            g, q = divmod(u, CHUNKS)
+        def store_codes(u, c0, c1):
+            g, q = ORDER[u]
             nc.sync.dma_start(
-                out=words_out[g][:, :, q * CHUNK : (q + 1) * CHUNK],
-                in_=y_codes[u][:].bitcast(I32).rearrange("p (c f) -> p c f", c=2),
+                out=words_out[g][:, c0:c1, q * CHUNK : (q + 1) * CHUNK],
+                in_=y_codes[u][:].bitcast(I32).rearrange("p (c f) -> p c f", c=2)[:, c0:c1, :],
             )
 
         def store_scale_rows(g, q0, q1, queues):
@@ -223,47 +240,61 @@ def tile_lucas_kanade_window_flow_k2_kernel(tc, window, g_words, g_scales, sxy, 
                     out=rows_out[g, r][:, :, q0 * w : q1 * w], in_=plane[r:P:32, :, q0 * w : q1 * w]
                 )
 
+        for j in range(FIRST):
+            sort_words(j)
+            turn(j)
+            if j < 2:
+                group_window(j)
+        quantize_window(0)
+        group_window(2)
+        sort_scales(0)
+        quantize_window(1)
+        quantize_window(2)
+
         last = UNITS - 1
         for s in range(STEPS + 1):
             tiles = TURN_BEFORE.get(s, [])
             for j in tiles:
                 turn(j)
             u, phase = divmod(s - PACK - 1, PACK)
+            for j in SORT_WORDS.get(s, []):
+                sort_words(j)
             if s > 0:
                 scale_sums(s - 1)
+            for j in GROUP_IN.get(s, []):
+                group_window(j)
             if u >= 0 and phase < 3:
                 interleave(u, SCALAR_COLS[phase], nc.scalar.copy)
             if s > 0:
                 solve(s - 1)
+            for j in QUANTIZE_IN.get(s, []):
+                quantize_window(j)
             if u >= 0 and phase == 0:
                 interleave(u, VECTOR_COLS, nc.vector.tensor_copy)
             if u >= 0 and phase in (1, 2):
-                quantize_y(u, phase - 1)
+                quantize_y(u, (phase - 1) * CHUNK, phase * CHUNK)
             if s in SORT_BEFORE:
                 sort_scales(SORT_BEFORE[s])
-            for j in tiles:
-                for h in range(2):
-                    quantize_window(j, h)
-                    if (j, h) == (0, 0):
-                        sort_scales(0)
             if s < STEPS:
                 multiply(s)
-            if s > 0 and s % PACK == 0 and s < STEPS:
+            if 0 < s <= FINE_FROM and s % PACK == 0:
                 store_y(s // PACK - 1, 0, PACK)
-            if s > last * PACK:
-                store_y(last, s - 1 - last * PACK, s - last * PACK)
+            if s > FINE_FROM:
+                store_y((s - 1) // PACK, (s - 1) % PACK, (s - 1) % PACK + 1)
             if u >= 0 and phase == 2:
-                store_codes(u)
-                if u == CHUNKS - 1:
-                    store_scale_rows(0, 0, CHUNKS, [nc.sync])
+                store_codes(u, 0, 2)
+                if u == CHUNKS:
+                    store_scale_rows(1, 0, CHUNKS, [nc.sync])
                 if u == last - 1:
-                    store_scale_rows(1, 0, CHUNKS - 1, [nc.sync])
+                    store_scale_rows(0, 0, CHUNKS - 1, [nc.sync])
 
         interleave(last, (0, 128), nc.scalar.copy)
         interleave(last, (128, 256), nc.vector.tensor_copy)
-        interleave(last, (400, 512), nc.scalar.copy)
-        interleave(last, (256, 400), nc.vector.tensor_copy)
-        quantize_y(last, 0)
-        quantize_y(last, 1)
-        store_codes(last)
-        store_scale_rows(1, CHUNKS - 1, CHUNKS, [nc.sync, nc.scalar])
+        interleave(last, (416, 512), nc.scalar.copy)
+        interleave(last, (256, 416), nc.vector.tensor_copy)
+        quantize_y(last, 0, 256)
+        store_codes(last, 0, 1)
+        quantize_y(last, 256, 384)
+        quantize_y(last, 384, 512)
+        store_codes(last, 1, 2)
+        store_scale_rows(0, CHUNKS - 1, CHUNKS, [nc.scalar, nc.sync])

@@ -35,9 +35,9 @@ SORT_WORDS = {1: [3], 2: [4], 3: [5], 4: [6], 5: [7]}
 GROUP_IN = TURN_BEFORE
 QUANTIZE_IN = TURN_BEFORE
 SORT_BEFORE = {4: 1, 8: 2, 12: 3}
-FINE_FROM = 16
-VECTOR_COLS = (0, 224)
-SCALAR_COLS = [(224, 320), (320, 416), (416, 512)]
+FINE_FROM = 24
+VECTOR_COLS = (0, 272)
+SCALAR_COLS = [(272, 352), (352, 432), (432, 512)]
 
 
 def tile_lucas_kanade_window_flow_k2_kernel(tc, window, g_words, g_scales, sxy, sopp, gain, out_0, out_1, out_2):
@@ -59,9 +59,8 @@ def tile_lucas_kanade_window_flow_k2_kernel(tc, window, g_words, g_scales, sxy, 
         y_codes = [keep.tile([P, N], U32, name="y_codes%d" % u, align_bytes=64) for u in range(UNITS)]
         y_planes = [keep.tile([P, 2 * FRAMES], U8, name="y_planes%d" % g, align_bytes=64) for g in range(GROUPS)]
         ident = keep.tile([P, P], F32, name="ident")
-        sxy_sb = keep.tile([P, GROUPS, PACK], BF16, name="sxy_sb")
-        gain_sb = keep.tile([P, GROUPS, PACK], BF16, name="gain_sb")
-        sopp_sb = keep.tile([P, GROUPS, PACK * 2], BF16, name="sopp_sb")
+        factor_rows = keep.tile([64, 2 * PACK * P], BF16, name="factor_rows")
+        factor_words = keep.tile([P, PACK, P], F32, name="factor_words")
         minus_gain = keep.tile([P, GROUPS * PACK], F32, name="minus_gain")
         cross = keep.tile([P, GROUPS * PACK], F32, name="cross")
         own = keep.tile([P, 2, GROUPS * PACK], F32, name="own")
@@ -91,12 +90,13 @@ def tile_lucas_kanade_window_flow_k2_kernel(tc, window, g_words, g_scales, sxy, 
             for r in range(4):
                 nc.sync.dma_start(out=g_rows[r:P:32, :, first:last], in_=rows_in[r][:, :, first:last])
 
-        nc.scalar.dma_start(out=gain_sb[:], in_=gain.rearrange("(g p t) -> p g t", g=GROUPS, t=PACK))
+        nc.scalar.dma_start(out=factor_rows[0:2, 0 : PACK * P], in_=sxy.rearrange("(g w) -> g w", g=GROUPS))
+        nc.scalar.dma_start(out=factor_rows[2:4, 0 : PACK * P], in_=gain.rearrange("(g w) -> g w", g=GROUPS))
+        nc.scalar.dma_start(out=factor_rows[32:34, :], in_=sopp.rearrange("(g w) c -> g (w c)", g=GROUPS))
+        nc.gpsimd.memset(factor_words[:], 0.0)
         nc.vector.memset(g_rows[:, :, 0:EARLY], 0)
         nc.vector.memset(g_rows[:, :, EARLY:ROW], 0)
         make_identity(nc, ident[:])
-        nc.gpsimd.dma_start(out=sxy_sb[:], in_=sxy.rearrange("(g p t) -> p g t", g=GROUPS, t=PACK))
-        nc.gpsimd.dma_start(out=sopp_sb[:], in_=sopp.rearrange("(g p t) c -> p g (t c)", g=GROUPS, t=PACK))
 
         for j in range(FIRST):
             load_window(j)
@@ -110,12 +110,40 @@ def tile_lucas_kanade_window_flow_k2_kernel(tc, window, g_words, g_scales, sxy, 
         load_chunk(2)
         load_chunk(3)
 
-        flat_gain = gain_sb[:].rearrange("p g t -> p (g t)")
-        nc.scalar.activation(out=minus_gain[:], in_=flat_gain, func=ACT.Copy, scale=-1.0)
-        nc.gpsimd.tensor_tensor(out=cross[:], in0=sxy_sb[:].rearrange("p g t -> p (g t)"), in1=flat_gain, op=ALU.mult)
-        sopp_by_c = sopp_sb[:].rearrange("p g (t c) -> p c (g t)", c=2)
-        for c in range(2):
-            nc.gpsimd.tensor_tensor(out=own[:, c, :], in0=sopp_by_c[:, c, :], in1=minus_gain[:], op=ALU.mult)
+        nc.vector.tensor_copy(
+            out=factor_words[0:4, 0:2, :],
+            in_=factor_rows[0:4, 0 : PACK * P].bitcast(F32).rearrange("r (p u) -> r u p", u=2),
+        )
+        nc.vector.tensor_copy(
+            out=factor_words[32:34, :, :], in_=factor_rows[32:34, :].bitcast(F32).rearrange("r (p t) -> r t p", t=PACK)
+        )
+        factor_bank = turn_ps.tile([P, PACK, P], F32, name="bank")
+        for t in range(PACK):
+            nc.tensor.transpose(factor_bank[:, t, :], factor_words[:, t, :], ident[:])
+        factors = factor_bank[:].bitcast(BF16)
+        by_window = "p (g u e) -> p g u e"
+        nc.scalar.activation(
+            out=minus_gain[:].rearrange(by_window, g=GROUPS, u=2),
+            in_=factors[:, 0:2, 4:8].rearrange("p u (g e) -> p g u e", g=GROUPS),
+            func=ACT.Copy,
+            scale=-1.0,
+        )
+
+        def make_factors():
+            nc.vector.tensor_tensor(
+                out=cross[:].rearrange(by_window, g=GROUPS, u=2),
+                in0=factors[:, 0:2, 0:4].rearrange("p u (g e) -> p g u e", g=GROUPS),
+                in1=minus_gain[:].rearrange(by_window, g=GROUPS, u=2),
+                op=ALU.mult,
+            )
+            sopp_by_c = factors[:, :, 64:68].rearrange("p t (g c) -> p c g t", g=GROUPS)
+            for c in range(2):
+                nc.vector.tensor_tensor(
+                    out=own[:, c, :].rearrange("p (g t) -> p g t", g=GROUPS),
+                    in0=sopp_by_c[:, c],
+                    in1=minus_gain[:].rearrange("p (g t) -> p g t", g=GROUPS),
+                    op=ALU.mult,
+                )
 
         ordered = {}
         turned = {}
@@ -196,7 +224,7 @@ def tile_lucas_kanade_window_flow_k2_kernel(tc, window, g_words, g_scales, sxy, 
                     scalar=own[:, c, j : j + 1],
                     in1=scaled[s][:, (1 - c) * CHUNK : (2 - c) * CHUNK],
                     op0=ALU.mult,
-                    op1=ALU.add,
+                    op1=ALU.subtract,
                 )
 
         def interleave(u, cols, copy):
@@ -242,6 +270,8 @@ def tile_lucas_kanade_window_flow_k2_kernel(tc, window, g_words, g_scales, sxy, 
 
         for j in range(FIRST):
             sort_words(j)
+            if j == 0:
+                make_factors()
             turn(j)
             if j < 2:
                 group_window(j)

@@ -35,7 +35,6 @@ SORT_WORDS = {1: [3], 2: [4], 3: [5], 4: [6], 5: [7]}
 GROUP_IN = TURN_BEFORE
 QUANTIZE_IN = TURN_BEFORE
 SORT_BEFORE = {4: 1, 8: 2, 12: 3}
-FINE_FROM = 24
 VECTOR_COLS = (0, 272)
 SCALAR_COLS = [(272, 352), (352, 432), (432, 512)]
 
@@ -90,9 +89,9 @@ def tile_lucas_kanade_window_flow_k2_kernel(tc, window, g_words, g_scales, sxy, 
             for r in range(4):
                 nc.sync.dma_start(out=g_rows[r:P:32, :, first:last], in_=rows_in[r][:, :, first:last])
 
-        nc.scalar.dma_start(out=factor_rows[0:2, 0 : PACK * P], in_=sxy.rearrange("(g w) -> g w", g=GROUPS))
-        nc.scalar.dma_start(out=factor_rows[2:4, 0 : PACK * P], in_=gain.rearrange("(g w) -> g w", g=GROUPS))
-        nc.scalar.dma_start(out=factor_rows[32:34, :], in_=sopp.rearrange("(g w) c -> g (w c)", g=GROUPS))
+        nc.sync.dma_start(out=factor_rows[0:2, 0 : PACK * P], in_=sxy.rearrange("(g w) -> g w", g=GROUPS))
+        nc.sync.dma_start(out=factor_rows[2:4, 0 : PACK * P], in_=gain.rearrange("(g w) -> g w", g=GROUPS))
+        nc.sync.dma_start(out=factor_rows[32:34, :], in_=sopp.rearrange("(g w) c -> g (w c)", g=GROUPS))
         nc.gpsimd.memset(factor_words[:], 0.0)
         nc.vector.memset(g_rows[:, :, 0:EARLY], 0)
         nc.vector.memset(g_rows[:, :, EARLY:ROW], 0)
@@ -307,16 +306,14 @@ def tile_lucas_kanade_window_flow_k2_kernel(tc, window, g_words, g_scales, sxy, 
                 sort_scales(SORT_BEFORE[s])
             if s < STEPS:
                 multiply(s)
-            if 0 < s <= FINE_FROM and s % PACK == 0:
-                store_y(s // PACK - 1, 0, PACK)
-            if s > FINE_FROM:
-                store_y((s - 1) // PACK, (s - 1) % PACK, (s - 1) % PACK + 1)
+            if s > 0 and s % 2 == 0:
+                store_y((s - 2) // PACK, (s - 2) % PACK, (s - 2) % PACK + 2)
             if u >= 0 and phase == 2:
                 store_codes(u, 0, 2)
                 if u == CHUNKS:
                     store_scale_rows(1, 0, CHUNKS, [nc.sync])
-                if u == last - 1:
-                    store_scale_rows(0, 0, CHUNKS - 1, [nc.sync])
+                if u == last - 2:
+                    store_scale_rows(0, 0, 2, [nc.sync])
 
         interleave(last, (0, 128), nc.scalar.copy)
         interleave(last, (128, 256), nc.vector.tensor_copy)
@@ -327,4 +324,4 @@ def tile_lucas_kanade_window_flow_k2_kernel(tc, window, g_words, g_scales, sxy, 
         quantize_y(last, 256, 384)
         quantize_y(last, 384, 512)
         store_codes(last, 1, 2)
-        store_scale_rows(0, CHUNKS - 1, CHUNKS, [nc.scalar, nc.sync])
+        store_scale_rows(0, 2, CHUNKS, [nc.scalar, nc.sync])

@@ -17,29 +17,40 @@ ALU = mybir.AluOpType
 ACT = mybir.ActivationFunctionType
 
 P = 128
+QUADRANT = 32
 PACK = 4
-GROUPS = 2
-PASSES = 4
+GROUPS = WINDOWS // (P * PACK)
+TILES = GROUPS * PACK
+PASSES = PIXELS // (P * PACK)
 CHUNK = 256
 CHUNKS = FRAMES // CHUNK
 N = 2 * CHUNK
+HALF = FRAMES // 2
 UNITS = GROUPS * CHUNKS
 STEPS = UNITS * PACK
-EARLY = (FRAMES + CHUNK) // 4
-ROW = 2 * FRAMES // 4
 
-ORDER = [(0, 0)] + [(1, q) for q in range(CHUNKS)] + [(0, q) for q in range(1, CHUNKS)]
-FIRST = 3
-TURN_BEFORE = {2: [3], 3: [4], 4: [5], 5: [6], 6: [7]}
-SORT_WORDS = {1: [3], 2: [4], 3: [5], 4: [6], 5: [7]}
-GROUP_IN = TURN_BEFORE
-QUANTIZE_IN = TURN_BEFORE
-SORT_BEFORE = {4: 1, 8: 2, 12: 3}
-VECTOR_COLS = (0, 272)
-SCALAR_COLS = [(272, 352), (352, 432), (432, 512)]
+ORDER = [(g, 2 * h + q) for h in range(2) for g in range(GROUPS) for q in range(2)]
+
+SCALE_ROW = 2 * FRAMES // PACK
+SCALE_CHUNK_0 = (FRAMES + CHUNK) // PACK
+SCALE_CHUNK_1 = (FRAMES + HALF) // PACK
+
+READY_AT_START = 3
+TURN_BEFORE_STEP = {2: 3, 6: 4, 7: 5, 8: 6, 9: 7}
+PLANE_BEFORE_STEP = {2: 1, 12: 2, 16: 3}
+
+VECTOR_COLS = (0, 256)
+SCALAR_COLS = [(256, 352), (352, 432), (432, 512)]
+LAST_SCALAR_COLS = [(0, 128), (416, 512)]
+LAST_VECTOR_COLS = [(128, 256), (256, 416)]
+LAST_QUANTIZE_CUT = 384
+
+SXY_ROW, GAIN_ROW, SOPP_ROW = 0, GROUPS, QUADRANT
 
 
-def tile_lucas_kanade_window_flow_k2_kernel(tc, window, g_words, g_scales, sxy, sopp, gain, out_0, out_1, out_2):
+def tile_lucas_kanade_window_flow_k2_kernel(
+    tc, window, g_words, g_scales, sxy, sopp, gain, out_0, out_1, out_2
+):
     nc = tc.nc
     with ExitStack() as ctx:
         keep = ctx.enter_context(tc.tile_pool(name="keep", bufs=1))
@@ -48,32 +59,33 @@ def tile_lucas_kanade_window_flow_k2_kernel(tc, window, g_words, g_scales, sxy, 
         sum_ps = ctx.enter_context(tc.psum_pool(name="sum_ps", bufs=4))
         ctx.enter_context(tc.manual_schedule())
 
-        w_raw = [keep.tile([P, PIXELS], BF16, name="w_raw%d" % j) for j in range(GROUPS * PACK)]
-        w_codes = [keep.tile([P, PASSES * P], U32, name="w_codes%d" % j, align_bytes=64) for j in range(GROUPS * PACK)]
-        w_scales = [keep.tile([P, PASSES * P], U8, name="w_scales%d" % j, align_bytes=64) for j in range(GROUPS * PACK)]
+        w_raw = [keep.tile([P, PIXELS], BF16, name="w_raw%d" % j) for j in range(TILES)]
+        w_codes = [keep.tile([P, PASSES * P], U32, name="w_codes%d" % j, align_bytes=64) for j in range(TILES)]
+        w_scales = [keep.tile([P, PASSES * P], U8, name="w_scales%d" % j, align_bytes=64) for j in range(TILES)]
         g_codes = [keep.tile([P, PASSES, N], U32, name="g_codes%d" % q, align_bytes=64) for q in range(CHUNKS)]
         g_planes = [keep.tile([P, PASSES, N], U8, name="g_planes%d" % q, align_bytes=64) for q in range(CHUNKS)]
-        g_rows = keep.tile([P, PASSES, ROW], I32, name="g_rows")
-        y = [keep.tile([P, PACK, N], F32, name="y%d" % u) for u in range(UNITS)]
-        y_codes = [keep.tile([P, N], U32, name="y_codes%d" % u, align_bytes=64) for u in range(UNITS)]
-        y_planes = [keep.tile([P, 2 * FRAMES], U8, name="y_planes%d" % g, align_bytes=64) for g in range(GROUPS)]
+        g_rows = keep.tile([P, PASSES, SCALE_ROW], I32, name="g_rows")
+        halves = [(g, h) for g in range(GROUPS) for h in range(2)]
+        y = {gh: keep.tile([P, PACK, 2, HALF], F32, name="y%d%d" % gh) for gh in halves}
+        y_codes = {gh: keep.tile([P, 2, HALF], U32, name="y_codes%d%d" % gh, align_bytes=64) for gh in halves}
+        y_planes = [keep.tile([P, HALF], U8, name="y_planes%d" % g, align_bytes=64) for g in range(GROUPS)]
         ident = keep.tile([P, P], F32, name="ident")
-        factor_rows = keep.tile([64, 2 * PACK * P], BF16, name="factor_rows")
+        factor_rows = keep.tile([2 * QUADRANT, 2 * PACK * P], BF16, name="factor_rows")
         factor_words = keep.tile([P, PACK, P], F32, name="factor_words")
-        minus_gain = keep.tile([P, GROUPS * PACK], F32, name="minus_gain")
-        cross = keep.tile([P, GROUPS * PACK], F32, name="cross")
-        own = keep.tile([P, 2, GROUPS * PACK], F32, name="own")
+        minus_gain = keep.tile([P, TILES], F32, name="minus_gain")
+        minus_cross = keep.tile([P, TILES], F32, name="minus_cross")
+        minus_own = keep.tile([P, 2, TILES], F32, name="minus_own")
 
+        window_in = window.rearrange("(g m t) k -> g t m k", g=GROUPS, t=PACK)
         words_in = g_words.rearrange("k p n t -> k p (n t)").bitcast(I32)
         rows_in = g_scales.bitcast(I32).rearrange("k (Q r) n -> r Q k n", r=4)
         y_out = out_0.rearrange("(g p t) c f -> g p (t c) f", g=GROUPS, t=PACK)
         words_out = out_1.rearrange("g p m t -> g p (m t)").bitcast(I32).rearrange("g p (c f) -> g p c f", c=2)
-        rows_out = out_2.bitcast(I32).rearrange("g (Q r) (c f) -> g r Q c f", r=4, c=2)
+        rows_out = out_2.bitcast(I32).rearrange("g (Q r) (plane f) -> g Q plane r f", r=4, plane=4)
 
         def load_window(j):
             g, t = divmod(j, PACK)
-            rows = window.rearrange("(g m t) k -> g t m k", g=GROUPS, t=PACK)
-            nc.sync.dma_start(out=w_raw[j][:], in_=rows[g, t])
+            nc.sync.dma_start(out=w_raw[j][:], in_=window_in[g, t])
 
         def load_pass(q, k):
             src = words_in[k].rearrange("p (c f) -> p c f", c=2)[:, :, q * CHUNK : (q + 1) * CHUNK]
@@ -85,114 +97,134 @@ def tile_lucas_kanade_window_flow_k2_kernel(tc, window, g_words, g_scales, sxy, 
                 src = words_in.rearrange("k p n -> p k n")[:, :, first : first + CHUNK]
                 nc.sync.dma_start(out=g_codes[q][:].bitcast(I32)[:, :, c * CHUNK : (c + 1) * CHUNK], in_=src)
 
-        def load_scale_rows(first, last):
+        def load_scale_rows(first, end):
             for r in range(4):
-                nc.sync.dma_start(out=g_rows[r:P:32, :, first:last], in_=rows_in[r][:, :, first:last])
+                nc.sync.dma_start(out=g_rows[r:P:QUADRANT, :, first:end], in_=rows_in[r][:, :, first:end])
 
-        nc.sync.dma_start(out=factor_rows[0:2, 0 : PACK * P], in_=sxy.rearrange("(g w) -> g w", g=GROUPS))
-        nc.sync.dma_start(out=factor_rows[2:4, 0 : PACK * P], in_=gain.rearrange("(g w) -> g w", g=GROUPS))
-        nc.sync.dma_start(out=factor_rows[32:34, :], in_=sopp.rearrange("(g w) c -> g (w c)", g=GROUPS))
+        nc.sync.dma_start(
+            out=factor_rows[SXY_ROW : SXY_ROW + GROUPS, 0 : PACK * P], in_=sxy.rearrange("(g w) -> g w", g=GROUPS)
+        )
+        nc.sync.dma_start(
+            out=factor_rows[GAIN_ROW : GAIN_ROW + GROUPS, 0 : PACK * P], in_=gain.rearrange("(g w) -> g w", g=GROUPS)
+        )
+        nc.sync.dma_start(
+            out=factor_rows[SOPP_ROW : SOPP_ROW + GROUPS, :], in_=sopp.rearrange("(g w) c -> g (w c)", g=GROUPS)
+        )
         nc.gpsimd.memset(factor_words[:], 0.0)
-        nc.vector.memset(g_rows[:, :, 0:EARLY], 0)
-        nc.vector.memset(g_rows[:, :, EARLY:ROW], 0)
+        nc.vector.memset(g_rows[:, :, 0:SCALE_CHUNK_0], 0)
+        nc.vector.memset(g_rows[:, :, SCALE_CHUNK_0:SCALE_ROW], 0)
         make_identity(nc, ident[:])
 
-        for j in range(FIRST):
+        for j in range(READY_AT_START):
             load_window(j)
-        load_scale_rows(0, EARLY)
+        load_scale_rows(0, SCALE_CHUNK_0)
         for k in range(PASSES):
             load_pass(0, k)
-        for j in range(FIRST, GROUPS * PACK):
-            load_window(j)
-        load_scale_rows(EARLY, ROW)
+        load_window(READY_AT_START)
+        load_scale_rows(SCALE_CHUNK_0, SCALE_CHUNK_1)
         load_chunk(1)
+        for j in range(PACK, TILES):
+            load_window(j)
+        load_scale_rows(SCALE_CHUNK_1, SCALE_ROW)
         load_chunk(2)
         load_chunk(3)
 
         nc.vector.tensor_copy(
-            out=factor_words[0:4, 0:2, :],
-            in_=factor_rows[0:4, 0 : PACK * P].bitcast(F32).rearrange("r (p u) -> r u p", u=2),
+            out=factor_words[0 : 2 * GROUPS, 0:2, :],
+            in_=factor_rows[0 : 2 * GROUPS, 0 : PACK * P].bitcast(F32).rearrange("r (p u) -> r u p", u=2),
         )
         nc.vector.tensor_copy(
-            out=factor_words[32:34, :, :], in_=factor_rows[32:34, :].bitcast(F32).rearrange("r (p t) -> r t p", t=PACK)
+            out=factor_words[SOPP_ROW : SOPP_ROW + GROUPS, :, :],
+            in_=factor_rows[SOPP_ROW : SOPP_ROW + GROUPS, :].bitcast(F32).rearrange("r (p t) -> r t p", t=PACK),
         )
         factor_bank = turn_ps.tile([P, PACK, P], F32, name="bank")
         for t in range(PACK):
             nc.tensor.transpose(factor_bank[:, t, :], factor_words[:, t, :], ident[:])
         factors = factor_bank[:].bitcast(BF16)
-        by_window = "p (g u e) -> p g u e"
+
+        def factor_pairs(row):
+            return factors[:, :, 2 * row : 2 * (row + GROUPS)].rearrange("p s (g e) -> p g s e", g=GROUPS)
+
+        def by_pair(columns):
+            return columns.rearrange("p (g u e) -> p g u e", g=GROUPS, u=2)
+
+        def by_group(columns):
+            return columns.rearrange("p (g t) -> p g t", g=GROUPS)
+
         nc.scalar.activation(
-            out=minus_gain[:].rearrange(by_window, g=GROUPS, u=2),
-            in_=factors[:, 0:2, 4:8].rearrange("p u (g e) -> p g u e", g=GROUPS),
-            func=ACT.Copy,
-            scale=-1.0,
+            out=by_pair(minus_gain[:]), in_=factor_pairs(GAIN_ROW)[:, :, 0:2, :], func=ACT.Copy, scale=-1.0
         )
 
-        def make_factors():
+        def multiply_factors():
             nc.vector.tensor_tensor(
-                out=cross[:].rearrange(by_window, g=GROUPS, u=2),
-                in0=factors[:, 0:2, 0:4].rearrange("p u (g e) -> p g u e", g=GROUPS),
-                in1=minus_gain[:].rearrange(by_window, g=GROUPS, u=2),
+                out=by_pair(minus_cross[:]),
+                in0=factor_pairs(SXY_ROW)[:, :, 0:2, :],
+                in1=by_pair(minus_gain[:]),
                 op=ALU.mult,
             )
-            sopp_by_c = factors[:, :, 64:68].rearrange("p t (g c) -> p c g t", g=GROUPS)
             for c in range(2):
                 nc.vector.tensor_tensor(
-                    out=own[:, c, :].rearrange("p (g t) -> p g t", g=GROUPS),
-                    in0=sopp_by_c[:, c],
-                    in1=minus_gain[:].rearrange("p (g t) -> p g t", g=GROUPS),
+                    out=by_group(minus_own[:, c, :]),
+                    in0=factor_pairs(SOPP_ROW)[:, :, :, c],
+                    in1=by_group(minus_gain[:]),
                     op=ALU.mult,
                 )
 
-        ordered = {}
-        turned = {}
-        grouped = {}
+        sorted_words = {}
+        turned_words = {}
+        grouped_words = {}
         sums = {}
-        scaled = {}
-        rounded = {}
+        crossed_sums = {}
+        rounded_y = {}
 
         def sort_words(j):
-            words = w_raw[j][:].bitcast(F32).rearrange("m (h k n i u) -> m h k n u i", h=2, k=2, i=4, u=2)
-            for h in range(2):
+            words = w_raw[j][:].bitcast(F32).rearrange("m (i k n w u) -> m i k n u w", i=2, k=2, w=4, u=2)
+            for i in range(2):
                 by_parity = ring.tile([P, 2, 2, P], F32, name="by_parity", bufs=4)
-                ordered[j, h] = by_parity
-                nc.vector.tensor_copy(out=by_parity[:].rearrange("m k u (n i) -> m k n u i", i=4), in_=words[:, h])
+                sorted_words[j, i] = by_parity
+                nc.vector.tensor_copy(out=by_parity[:].rearrange("m k u (n w) -> m k n u w", w=4), in_=words[:, i])
 
         def turn(j):
-            for h in range(2):
+            for i in range(2):
                 bank = turn_ps.tile([P, 2, 2, P], F32, name="bank")
-                turned[j, h] = bank
+                turned_words[j, i] = bank
                 for k in range(2):
                     for u in range(2):
-                        nc.tensor.transpose(bank[:, k, u, :], ordered[j, h][:, k, u, :], ident[:])
+                        nc.tensor.transpose(bank[:, k, u, :], sorted_words[j, i][:, k, u, :], ident[:])
 
-        def group_window(j):
-            for h in range(2):
+        def group_words(j):
+            for i in range(2):
                 fours = ring.tile([P, 2 * P * PACK], BF16, name="fours", align_bytes=64, bufs=4)
-                grouped[j, h] = fours
+                grouped_words[j, i] = fours
                 nc.scalar.copy(
                     out=fours[:].bitcast(F32).rearrange("p (k m u) -> p k m u", k=2, u=2),
-                    in_=turned[j, h][:].rearrange("p k u m -> p k m u"),
+                    in_=turned_words[j, i][:].rearrange("p k u m -> p k m u"),
                 )
 
         def quantize_window(j):
-            for h in range(2):
-                cols = slice(h * 2 * P, (h + 1) * 2 * P)
+            for i in range(2):
+                cols = slice(i * 2 * P, (i + 1) * 2 * P)
                 nc.vector.quantize_mx(
-                    out=w_codes[j][:, cols].bitcast(E4M3X4), scales=w_scales[j][:, cols], in_=grouped[j, h][:]
+                    out=w_codes[j][:, cols].bitcast(E4M3X4), scales=w_scales[j][:, cols], in_=grouped_words[j, i][:]
                 )
 
-        def sort_scales(q):
-            w = CHUNK // 4
+        def lay_plane(q):
+            width = CHUNK // PACK
             nc.vector.tensor_copy(
                 out=g_planes[q][:].bitcast(I32).rearrange("p k (c f) -> p k c f", c=2),
-                in_=g_rows[:].rearrange("p k (c f) -> p k c f", c=2)[:, :, :, q * w : (q + 1) * w],
+                in_=g_rows[:].rearrange("p k (c f) -> p k c f", c=2)[:, :, :, q * width : (q + 1) * width],
             )
 
+        def tile_of(s):
+            return ORDER[s // PACK][0] * PACK + s % PACK
+
+        def place(unit):
+            g, q = ORDER[unit]
+            return g, q // 2, (q % 2) * CHUNK
+
         def multiply(s):
-            u, t = divmod(s, PACK)
-            g, q = ORDER[u]
-            j = g * PACK + t
+            q = ORDER[s // PACK][1]
+            j = tile_of(s)
             acc = sum_ps.tile([P, N], F32, name="acc")
             sums[s] = acc
             for k in range(PASSES):
@@ -207,121 +239,137 @@ def tile_lucas_kanade_window_flow_k2_kernel(tc, window, g_words, g_scales, sxy, 
                     stop=(k == PASSES - 1),
                 )
 
-        def scale_sums(s):
-            j = ORDER[s // PACK][0] * PACK + s % PACK
+        def cross_sums(s):
+            j = tile_of(s)
             crossed = ring.tile([P, N], F32, name="crossed")
-            scaled[s] = crossed
-            nc.scalar.activation(out=crossed[:], in_=sums[s][:], func=ACT.Copy, scale=cross[:, j : j + 1])
+            crossed_sums[s] = crossed
+            nc.scalar.activation(out=crossed[:], in_=sums[s][:], func=ACT.Copy, scale=minus_cross[:, j : j + 1])
 
         def solve(s):
-            u, t = divmod(s, PACK)
-            j = ORDER[u][0] * PACK + t
+            unit, t = divmod(s, PACK)
+            g, h, f = place(unit)
+            j = tile_of(s)
             for c in range(2):
                 nc.vector.scalar_tensor_tensor(
-                    out=y[u][:, t, c * CHUNK : (c + 1) * CHUNK],
+                    out=y[g, h][:, t, c, f : f + CHUNK],
                     in0=sums[s][:, c * CHUNK : (c + 1) * CHUNK],
-                    scalar=own[:, c, j : j + 1],
-                    in1=scaled[s][:, (1 - c) * CHUNK : (2 - c) * CHUNK],
+                    scalar=minus_own[:, c, j : j + 1],
+                    in1=crossed_sums[s][:, (1 - c) * CHUNK : (2 - c) * CHUNK],
                     op0=ALU.mult,
                     op1=ALU.subtract,
                 )
 
-        def interleave(u, cols, copy):
-            if u not in rounded:
-                rounded[u] = ring.tile([P, N, PACK], BF16, name="rounded", align_bytes=64)
-            a, b = cols
+        def unit_columns(unit, cols):
+            g, h, f = place(unit)
+            c, first = divmod(cols[0], CHUNK)
+            return g, h, c, slice(f + first, f + first + cols[1] - cols[0])
+
+        def interleave(unit, cols, copy):
+            if unit not in rounded_y:
+                rounded_y[unit] = ring.tile([P, N, PACK], BF16, name="rounded", align_bytes=64)
+            g, h, c, frames = unit_columns(unit, cols)
             copy(
-                out=rounded[u][:, a:b, :].rearrange("p (n i) t -> p n t i", i=4),
-                in_=y[u][:, :, a:b].rearrange("p t (n i) -> p n t i", i=4),
+                out=rounded_y[unit][:, cols[0] : cols[1], :].rearrange("p (n w) t -> p n t w", w=4),
+                in_=y[g, h][:, :, c, frames].rearrange("p t (n w) -> p n t w", w=4),
             )
 
-        def quantize_y(u, a, b):
-            g, q = ORDER[u]
-            c, f = divmod(a, CHUNK)
-            first = c * FRAMES + q * CHUNK + f
+        def quantize_y(unit, cols):
+            g, h, c, frames = unit_columns(unit, cols)
             nc.vector.quantize_mx(
-                out=y_codes[u][:, a:b].bitcast(E4M3X4),
-                scales=y_planes[g][:, first : first + b - a],
-                in_=rounded[u][:, a:b, :].rearrange("p n t -> p (n t)"),
+                out=y_codes[g, h][:, c, frames].bitcast(E4M3X4),
+                scales=y_planes[g][4 * (2 * c + h) : P, frames],
+                in_=rounded_y[unit][:, cols[0] : cols[1], :].rearrange("p n t -> p (n t)"),
             )
 
-        def store_y(u, t0, t1):
-            g, q = ORDER[u]
+        def store_y(g, h, t0, t1, f0, f1):
             nc.sync.dma_start(
-                out=y_out[g][:, 2 * t0 : 2 * t1, q * CHUNK : (q + 1) * CHUNK],
-                in_=y[u][:, t0:t1, :].rearrange("p t (c f) -> p (t c) f", c=2),
+                out=y_out[g][:, 2 * t0 : 2 * t1, h * HALF + f0 : h * HALF + f1],
+                in_=y[g, h][:, t0:t1].rearrange("p t c f -> p (t c) f")[:, :, f0:f1],
             )
 
-        def store_codes(u, c0, c1):
-            g, q = ORDER[u]
+        def store_codes(g, h, c0, c1, f0, f1):
             nc.sync.dma_start(
-                out=words_out[g][:, c0:c1, q * CHUNK : (q + 1) * CHUNK],
-                in_=y_codes[u][:].bitcast(I32).rearrange("p (c f) -> p c f", c=2)[:, c0:c1, :],
+                out=words_out[g][:, c0:c1, h * HALF + f0 : h * HALF + f1],
+                in_=y_codes[g, h][:].bitcast(I32)[:, c0:c1, f0:f1],
             )
 
-        def store_scale_rows(g, q0, q1, queues):
-            w = CHUNK // 4
-            plane = y_planes[g][:].bitcast(I32).rearrange("p (c f) -> p c f", c=2)
-            for r in range(4):
-                queues[r % len(queues)].dma_start(
-                    out=rows_out[g, r][:, :, q0 * w : q1 * w], in_=plane[r:P:32, :, q0 * w : q1 * w]
+        def store_scale_rows(g, queues):
+            for Q in range(4):
+                queues[Q % len(queues)].dma_start(
+                    out=rows_out[g, Q], in_=y_planes[g][:].bitcast(I32)[QUADRANT * Q : QUADRANT * Q + 16, :]
                 )
 
-        for j in range(FIRST):
-            sort_words(j)
-            if j == 0:
-                make_factors()
-            turn(j)
-            if j < 2:
-                group_window(j)
+        def store_after_step(s):
+            unit, t = divmod(s, PACK)
+            g, h, f = place(unit)
+            if h == 0 and f > 0:
+                store_y(g, h, t, t + 1, 0, HALF)
+            if h == 1 and t % 2 == 1:
+                store_y(g, h, t - 1, t + 1, f, f + CHUNK)
+
+        def store_after_unit(unit):
+            g, h, f = place(unit)
+            if h == 0 and f > 0:
+                store_codes(g, h, 0, 2, 0, HALF)
+            if h == 1:
+                store_codes(g, h, 0, 2, f, f + CHUNK)
+            if h == 1 and f > 0:
+                store_scale_rows(g, [nc.sync])
+
+        sort_words(0)
+        multiply_factors()
+        turn(0)
+        group_words(0)
+        sort_words(1)
+        turn(1)
+        group_words(1)
+        sort_words(2)
+        turn(2)
         quantize_window(0)
-        group_window(2)
-        sort_scales(0)
+        group_words(2)
+        lay_plane(0)
         quantize_window(1)
         quantize_window(2)
 
-        last = UNITS - 1
         for s in range(STEPS + 1):
-            tiles = TURN_BEFORE.get(s, [])
-            for j in tiles:
-                turn(j)
-            u, phase = divmod(s - PACK - 1, PACK)
-            for j in SORT_WORDS.get(s, []):
-                sort_words(j)
+            new_tile = TURN_BEFORE_STEP.get(s)
+            unit, phase = divmod(s - PACK - 1, PACK)
+            finishing = unit >= 0 and phase < len(SCALAR_COLS)
+            if new_tile is not None:
+                turn(new_tile)
+            if s + 1 in TURN_BEFORE_STEP:
+                sort_words(TURN_BEFORE_STEP[s + 1])
             if s > 0:
-                scale_sums(s - 1)
-            for j in GROUP_IN.get(s, []):
-                group_window(j)
-            if u >= 0 and phase < 3:
-                interleave(u, SCALAR_COLS[phase], nc.scalar.copy)
+                cross_sums(s - 1)
+            if new_tile is not None:
+                group_words(new_tile)
+            if finishing:
+                interleave(unit, SCALAR_COLS[phase], nc.scalar.copy)
             if s > 0:
                 solve(s - 1)
-            for j in QUANTIZE_IN.get(s, []):
-                quantize_window(j)
-            if u >= 0 and phase == 0:
-                interleave(u, VECTOR_COLS, nc.vector.tensor_copy)
-            if u >= 0 and phase in (1, 2):
-                quantize_y(u, (phase - 1) * CHUNK, phase * CHUNK)
-            if s in SORT_BEFORE:
-                sort_scales(SORT_BEFORE[s])
+            if new_tile is not None:
+                quantize_window(new_tile)
+            if finishing and phase == 0:
+                interleave(unit, VECTOR_COLS, nc.vector.tensor_copy)
+            if finishing and phase > 0:
+                quantize_y(unit, ((phase - 1) * CHUNK, phase * CHUNK))
+            if s in PLANE_BEFORE_STEP:
+                lay_plane(PLANE_BEFORE_STEP[s])
             if s < STEPS:
                 multiply(s)
-            if s > 0 and s % 2 == 0:
-                store_y((s - 2) // PACK, (s - 2) % PACK, (s - 2) % PACK + 2)
-            if u >= 0 and phase == 2:
-                store_codes(u, 0, 2)
-                if u == CHUNKS:
-                    store_scale_rows(1, 0, CHUNKS, [nc.sync])
-                if u == last - 2:
-                    store_scale_rows(0, 0, 2, [nc.sync])
+            if s > 0:
+                store_after_step(s - 1)
+            if finishing and phase == 2:
+                store_after_unit(unit)
 
-        interleave(last, (0, 128), nc.scalar.copy)
-        interleave(last, (128, 256), nc.vector.tensor_copy)
-        interleave(last, (416, 512), nc.scalar.copy)
-        interleave(last, (256, 416), nc.vector.tensor_copy)
-        quantize_y(last, 0, 256)
-        store_codes(last, 0, 1)
-        quantize_y(last, 256, 384)
-        quantize_y(last, 384, 512)
-        store_codes(last, 1, 2)
-        store_scale_rows(0, 2, CHUNKS, [nc.scalar, nc.sync])
+        last = UNITS - 1
+        g, h, f = place(last)
+        for c in range(2):
+            interleave(last, LAST_SCALAR_COLS[c], nc.scalar.copy)
+            interleave(last, LAST_VECTOR_COLS[c], nc.vector.tensor_copy)
+        quantize_y(last, (0, CHUNK))
+        store_codes(g, h, 0, 1, f, HALF)
+        quantize_y(last, (CHUNK, LAST_QUANTIZE_CUT))
+        quantize_y(last, (LAST_QUANTIZE_CUT, N))
+        store_codes(g, h, 1, 2, f, HALF)
+        store_scale_rows(g, [nc.scalar, nc.sync])

from contextlib import ExitStack

import concourse.mybir as mybir
from concourse.masks import make_identity

WINDOWS, PIXELS, FRAMES = 1024, 2048, 1024
FLOPS = 2 * WINDOWS * PIXELS * 2 * FRAMES

F32 = mybir.dt.float32
BF16 = mybir.dt.bfloat16
I32 = mybir.dt.int32
U32 = mybir.dt.uint32
U8 = mybir.dt.uint8
E4M3X4 = mybir.dt.float8_e4m3fn_x4
E5M2X4 = mybir.dt.float8_e5m2_x4
ALU = mybir.AluOpType
ACT = mybir.ActivationFunctionType

P = 128
QUADRANT = 32
PACK = 4
GROUPS = WINDOWS // (P * PACK)
TILES = GROUPS * PACK
PASSES = PIXELS // (P * PACK)
CHUNK = 256
CHUNKS = FRAMES // CHUNK
N = 2 * CHUNK
HALF = FRAMES // 2
UNITS = GROUPS * CHUNKS
STEPS = UNITS * PACK

ORDER = [(g, 2 * h + q) for h in range(2) for g in range(GROUPS) for q in range(2)]

SCALE_ROW = 2 * FRAMES // PACK
SCALE_CHUNK_0 = (FRAMES + CHUNK) // PACK
SCALE_CHUNK_1 = (FRAMES + HALF) // PACK

READY_AT_START = 3
TURN_BEFORE_STEP = {2: 3, 6: 4, 7: 5, 8: 6, 9: 7}
PLANE_BEFORE_STEP = {2: 1, 12: 2, 16: 3}

VECTOR_COLS = (0, 256)
SCALAR_COLS = [(256, 352), (352, 432), (432, 512)]
LAST_SCALAR_COLS = [(0, 128), (416, 512)]
LAST_VECTOR_COLS = [(128, 256), (256, 416)]
LAST_QUANTIZE_CUT = 384

SXY_ROW, GAIN_ROW, SOPP_ROW = 0, GROUPS, QUADRANT


def tile_lucas_kanade_window_flow_k2_kernel(
    tc, window, g_words, g_scales, sxy, sopp, gain, out_0, out_1, out_2
):
    nc = tc.nc
    with ExitStack() as ctx:
        keep = ctx.enter_context(tc.tile_pool(name="keep", bufs=1))
        ring = ctx.enter_context(tc.tile_pool(name="ring", bufs=3))
        turn_ps = ctx.enter_context(tc.psum_pool(name="turn_ps", bufs=4))
        sum_ps = ctx.enter_context(tc.psum_pool(name="sum_ps", bufs=4))
        ctx.enter_context(tc.manual_schedule())

        w_raw = [keep.tile([P, PIXELS], BF16, name="w_raw%d" % j) for j in range(TILES)]
        w_codes = [keep.tile([P, PASSES * P], U32, name="w_codes%d" % j, align_bytes=64) for j in range(TILES)]
        w_scales = [keep.tile([P, PASSES * P], U8, name="w_scales%d" % j, align_bytes=64) for j in range(TILES)]
        g_codes = [keep.tile([P, PASSES, N], U32, name="g_codes%d" % q, align_bytes=64) for q in range(CHUNKS)]
        g_planes = [keep.tile([P, PASSES, N], U8, name="g_planes%d" % q, align_bytes=64) for q in range(CHUNKS)]
        g_rows = keep.tile([P, PASSES, SCALE_ROW], I32, name="g_rows")
        halves = [(g, h) for g in range(GROUPS) for h in range(2)]
        y = {gh: keep.tile([P, PACK, 2, HALF], F32, name="y%d%d" % gh) for gh in halves}
        y_codes = {gh: keep.tile([P, 2, HALF], U32, name="y_codes%d%d" % gh, align_bytes=64) for gh in halves}
        y_planes = [keep.tile([P, HALF], U8, name="y_planes%d" % g, align_bytes=64) for g in range(GROUPS)]
        ident = keep.tile([P, P], F32, name="ident")
        factor_rows = keep.tile([2 * QUADRANT, 2 * PACK * P], BF16, name="factor_rows")
        factor_words = keep.tile([P, PACK, P], F32, name="factor_words")
        minus_gain = keep.tile([P, TILES], F32, name="minus_gain")
        minus_cross = keep.tile([P, TILES], F32, name="minus_cross")
        minus_own = keep.tile([P, 2, TILES], F32, name="minus_own")

        window_in = window.rearrange("(g m t) k -> g t m k", g=GROUPS, t=PACK)
        words_in = g_words.rearrange("k p n t -> k p (n t)").bitcast(I32)
        rows_in = g_scales.bitcast(I32).rearrange("k (Q r) n -> r Q k n", r=4)
        y_out = out_0.rearrange("(g p t) c f -> g p (t c) f", g=GROUPS, t=PACK)
        words_out = out_1.rearrange("g p m t -> g p (m t)").bitcast(I32).rearrange("g p (c f) -> g p c f", c=2)
        rows_out = out_2.bitcast(I32).rearrange("g (Q r) (plane f) -> g Q plane r f", r=4, plane=4)

        def load_window(j):
            g, t = divmod(j, PACK)
            nc.sync.dma_start(out=w_raw[j][:], in_=window_in[g, t])

        def load_pass(q, k):
            src = words_in[k].rearrange("p (c f) -> p c f", c=2)[:, :, q * CHUNK : (q + 1) * CHUNK]
            nc.sync.dma_start(out=g_codes[q][:, k, :].bitcast(I32).rearrange("p (c f) -> p c f", c=2), in_=src)

        def load_chunk(q):
            for c in range(2):
                first = c * FRAMES + q * CHUNK
                src = words_in.rearrange("k p n -> p k n")[:, :, first : first + CHUNK]
                nc.sync.dma_start(out=g_codes[q][:].bitcast(I32)[:, :, c * CHUNK : (c + 1) * CHUNK], in_=src)

        def load_scale_rows(first, end):
            for r in range(4):
                nc.sync.dma_start(out=g_rows[r:P:QUADRANT, :, first:end], in_=rows_in[r][:, :, first:end])

        nc.sync.dma_start(
            out=factor_rows[SXY_ROW : SXY_ROW + GROUPS, 0 : PACK * P], in_=sxy.rearrange("(g w) -> g w", g=GROUPS)
        )
        nc.sync.dma_start(
            out=factor_rows[GAIN_ROW : GAIN_ROW + GROUPS, 0 : PACK * P], in_=gain.rearrange("(g w) -> g w", g=GROUPS)
        )
        nc.sync.dma_start(
            out=factor_rows[SOPP_ROW : SOPP_ROW + GROUPS, :], in_=sopp.rearrange("(g w) c -> g (w c)", g=GROUPS)
        )
        nc.gpsimd.memset(factor_words[:], 0.0)
        nc.vector.memset(g_rows[:, :, 0:SCALE_CHUNK_0], 0)
        nc.vector.memset(g_rows[:, :, SCALE_CHUNK_0:SCALE_ROW], 0)
        make_identity(nc, ident[:])

        for j in range(READY_AT_START):
            load_window(j)
        load_scale_rows(0, SCALE_CHUNK_0)
        for k in range(PASSES):
            load_pass(0, k)
        load_window(READY_AT_START)
        load_scale_rows(SCALE_CHUNK_0, SCALE_CHUNK_1)
        load_chunk(1)
        for j in range(PACK, TILES):
            load_window(j)
        load_scale_rows(SCALE_CHUNK_1, SCALE_ROW)
        load_chunk(2)
        load_chunk(3)

        nc.vector.tensor_copy(
            out=factor_words[0 : 2 * GROUPS, 0:2, :],
            in_=factor_rows[0 : 2 * GROUPS, 0 : PACK * P].bitcast(F32).rearrange("r (p u) -> r u p", u=2),
        )
        nc.vector.tensor_copy(
            out=factor_words[SOPP_ROW : SOPP_ROW + GROUPS, :, :],
            in_=factor_rows[SOPP_ROW : SOPP_ROW + GROUPS, :].bitcast(F32).rearrange("r (p t) -> r t p", t=PACK),
        )
        factor_bank = turn_ps.tile([P, PACK, P], F32, name="bank")
        for t in range(PACK):
            nc.tensor.transpose(factor_bank[:, t, :], factor_words[:, t, :], ident[:])
        factors = factor_bank[:].bitcast(BF16)

        def factor_pairs(row):
            return factors[:, :, 2 * row : 2 * (row + GROUPS)].rearrange("p s (g e) -> p g s e", g=GROUPS)

        def by_pair(columns):
            return columns.rearrange("p (g u e) -> p g u e", g=GROUPS, u=2)

        def by_group(columns):
            return columns.rearrange("p (g t) -> p g t", g=GROUPS)

        nc.scalar.activation(
            out=by_pair(minus_gain[:]), in_=factor_pairs(GAIN_ROW)[:, :, 0:2, :], func=ACT.Copy, scale=-1.0
        )

        def multiply_factors():
            nc.vector.tensor_tensor(
                out=by_pair(minus_cross[:]),
                in0=factor_pairs(SXY_ROW)[:, :, 0:2, :],
                in1=by_pair(minus_gain[:]),
                op=ALU.mult,
            )
            for c in range(2):
                nc.vector.tensor_tensor(
                    out=by_group(minus_own[:, c, :]),
                    in0=factor_pairs(SOPP_ROW)[:, :, :, c],
                    in1=by_group(minus_gain[:]),
                    op=ALU.mult,
                )

        sorted_words = {}
        turned_words = {}
        grouped_words = {}
        sums = {}
        crossed_sums = {}
        rounded_y = {}

        def sort_words(j):
            words = w_raw[j][:].bitcast(F32).rearrange("m (i k n w u) -> m i k n u w", i=2, k=2, w=4, u=2)
            for i in range(2):
                by_parity = ring.tile([P, 2, 2, P], F32, name="by_parity", bufs=4)
                sorted_words[j, i] = by_parity
                nc.vector.tensor_copy(out=by_parity[:].rearrange("m k u (n w) -> m k n u w", w=4), in_=words[:, i])

        def turn(j):
            for i in range(2):
                bank = turn_ps.tile([P, 2, 2, P], F32, name="bank")
                turned_words[j, i] = bank
                for k in range(2):
                    for u in range(2):
                        nc.tensor.transpose(bank[:, k, u, :], sorted_words[j, i][:, k, u, :], ident[:])

        def group_words(j):
            for i in range(2):
                fours = ring.tile([P, 2 * P * PACK], BF16, name="fours", align_bytes=64, bufs=4)
                grouped_words[j, i] = fours
                nc.scalar.copy(
                    out=fours[:].bitcast(F32).rearrange("p (k m u) -> p k m u", k=2, u=2),
                    in_=turned_words[j, i][:].rearrange("p k u m -> p k m u"),
                )

        def quantize_window(j):
            for i in range(2):
                cols = slice(i * 2 * P, (i + 1) * 2 * P)
                nc.vector.quantize_mx(
                    out=w_codes[j][:, cols].bitcast(E4M3X4), scales=w_scales[j][:, cols], in_=grouped_words[j, i][:]
                )

        def lay_plane(q):
            width = CHUNK // PACK
            nc.vector.tensor_copy(
                out=g_planes[q][:].bitcast(I32).rearrange("p k (c f) -> p k c f", c=2),
                in_=g_rows[:].rearrange("p k (c f) -> p k c f", c=2)[:, :, :, q * width : (q + 1) * width],
            )

        def tile_of(s):
            return ORDER[s // PACK][0] * PACK + s % PACK

        def place(unit):
            g, q = ORDER[unit]
            return g, q // 2, (q % 2) * CHUNK

        def multiply(s):
            q = ORDER[s // PACK][1]
            j = tile_of(s)
            acc = sum_ps.tile([P, N], F32, name="acc")
            sums[s] = acc
            for k in range(PASSES):
                cols = slice(k * P, (k + 1) * P)
                nc.tensor.matmul_mx(
                    out=acc[:],
                    lhsT=w_codes[j][:, cols].bitcast(E4M3X4),
                    lhsT_scale=w_scales[j][:, cols],
                    rhs=g_codes[q][:, k, :].bitcast(E5M2X4),
                    rhs_scale=g_planes[q][:, k, :],
                    start=(k == 0),
                    stop=(k == PASSES - 1),
                )

        def cross_sums(s):
            j = tile_of(s)
            crossed = ring.tile([P, N], F32, name="crossed")
            crossed_sums[s] = crossed
            nc.scalar.activation(out=crossed[:], in_=sums[s][:], func=ACT.Copy, scale=minus_cross[:, j : j + 1])

        def solve(s):
            unit, t = divmod(s, PACK)
            g, h, f = place(unit)
            j = tile_of(s)
            for c in range(2):
                nc.vector.scalar_tensor_tensor(
                    out=y[g, h][:, t, c, f : f + CHUNK],
                    in0=sums[s][:, c * CHUNK : (c + 1) * CHUNK],
                    scalar=minus_own[:, c, j : j + 1],
                    in1=crossed_sums[s][:, (1 - c) * CHUNK : (2 - c) * CHUNK],
                    op0=ALU.mult,
                    op1=ALU.subtract,
                )

        def unit_columns(unit, cols):
            g, h, f = place(unit)
            c, first = divmod(cols[0], CHUNK)
            return g, h, c, slice(f + first, f + first + cols[1] - cols[0])

        def interleave(unit, cols, copy):
            if unit not in rounded_y:
                rounded_y[unit] = ring.tile([P, N, PACK], BF16, name="rounded", align_bytes=64)
            g, h, c, frames = unit_columns(unit, cols)
            copy(
                out=rounded_y[unit][:, cols[0] : cols[1], :].rearrange("p (n w) t -> p n t w", w=4),
                in_=y[g, h][:, :, c, frames].rearrange("p t (n w) -> p n t w", w=4),
            )

        def quantize_y(unit, cols):
            g, h, c, frames = unit_columns(unit, cols)
            nc.vector.quantize_mx(
                out=y_codes[g, h][:, c, frames].bitcast(E4M3X4),
                scales=y_planes[g][4 * (2 * c + h) : P, frames],
                in_=rounded_y[unit][:, cols[0] : cols[1], :].rearrange("p n t -> p (n t)"),
            )

        def store_y(g, h, t0, t1, f0, f1):
            nc.sync.dma_start(
                out=y_out[g][:, 2 * t0 : 2 * t1, h * HALF + f0 : h * HALF + f1],
                in_=y[g, h][:, t0:t1].rearrange("p t c f -> p (t c) f")[:, :, f0:f1],
            )

        def store_codes(g, h, c0, c1, f0, f1):
            nc.sync.dma_start(
                out=words_out[g][:, c0:c1, h * HALF + f0 : h * HALF + f1],
                in_=y_codes[g, h][:].bitcast(I32)[:, c0:c1, f0:f1],
            )

        def store_scale_rows(g, queues):
            for Q in range(4):
                queues[Q % len(queues)].dma_start(
                    out=rows_out[g, Q], in_=y_planes[g][:].bitcast(I32)[QUADRANT * Q : QUADRANT * Q + 16, :]
                )

        def store_after_step(s):
            unit, t = divmod(s, PACK)
            g, h, f = place(unit)
            if h == 0 and f > 0:
                store_y(g, h, t, t + 1, 0, HALF)
            if h == 1 and t % 2 == 1:
                store_y(g, h, t - 1, t + 1, f, f + CHUNK)

        def store_after_unit(unit):
            g, h, f = place(unit)
            if h == 0 and f > 0:
                store_codes(g, h, 0, 2, 0, HALF)
            if h == 1:
                store_codes(g, h, 0, 2, f, f + CHUNK)
            if h == 1 and f > 0:
                store_scale_rows(g, [nc.sync])

        sort_words(0)
        multiply_factors()
        turn(0)
        group_words(0)
        sort_words(1)
        turn(1)
        group_words(1)
        sort_words(2)
        turn(2)
        quantize_window(0)
        group_words(2)
        lay_plane(0)
        quantize_window(1)
        quantize_window(2)

        for s in range(STEPS + 1):
            new_tile = TURN_BEFORE_STEP.get(s)
            unit, phase = divmod(s - PACK - 1, PACK)
            finishing = unit >= 0 and phase < len(SCALAR_COLS)
            if new_tile is not None:
                turn(new_tile)
            if s + 1 in TURN_BEFORE_STEP:
                sort_words(TURN_BEFORE_STEP[s + 1])
            if s > 0:
                cross_sums(s - 1)
            if new_tile is not None:
                group_words(new_tile)
            if finishing:
                interleave(unit, SCALAR_COLS[phase], nc.scalar.copy)
            if s > 0:
                solve(s - 1)
            if new_tile is not None:
                quantize_window(new_tile)
            if finishing and phase == 0:
                interleave(unit, VECTOR_COLS, nc.vector.tensor_copy)
            if finishing and phase > 0:
                quantize_y(unit, ((phase - 1) * CHUNK, phase * CHUNK))
            if s in PLANE_BEFORE_STEP:
                lay_plane(PLANE_BEFORE_STEP[s])
            if s < STEPS:
                multiply(s)
            if s > 0:
                store_after_step(s - 1)
            if finishing and phase == 2:
                store_after_unit(unit)

        last = UNITS - 1
        g, h, f = place(last)
        for c in range(2):
            interleave(last, LAST_SCALAR_COLS[c], nc.scalar.copy)
            interleave(last, LAST_VECTOR_COLS[c], nc.vector.tensor_copy)
        quantize_y(last, (0, CHUNK))
        store_codes(g, h, 0, 1, f, HALF)
        quantize_y(last, (CHUNK, LAST_QUANTIZE_CUT))
        quantize_y(last, (LAST_QUANTIZE_CUT, N))
        store_codes(g, h, 1, 2, f, HALF)
        store_scale_rows(g, [nc.scalar, nc.sync])
